import numpy as np
import ml_dtypes


def mxq(x, axis, fmt="e4m3"):
    dtype, down = {"e4m3": (ml_dtypes.float8_e4m3fn, 7), "e5m2": (ml_dtypes.float8_e5m2, 14)}[fmt]
    v = np.moveaxis(np.asarray(x, np.float32).astype(ml_dtypes.bfloat16).astype(np.float64), axis, -1)
    blocks = v.reshape(v.shape[:-1] + (-1, 32))
    amax = np.abs(blocks).max(-1, keepdims=True)
    byte = np.maximum(np.where(amax > 0, np.frexp(amax)[1] - 1 + 127, 0) - down, 1)
    scale = np.exp2(byte - 127.0)
    codes = (blocks / scale).astype(np.float32).astype(dtype).astype(np.float64)
    return np.moveaxis((codes * scale).reshape(v.shape), -1, axis)


WIDE = False


def mx_kscale(k):
    if not WIDE:
        return np.ones(k)
    levels = np.array([10, -10, 5, -5, 0])
    if k % 512:
        return np.exp2(np.random.permutation(np.resize(levels, k // 32))).repeat(32)
    a = np.empty((k // 512, 16))
    for p in range(k // 512):
        a[p, :8] = np.random.permutation(np.resize(levels, 8))
        for g in range(8):
            far = levels[np.abs(levels - a[p, g]) >= 10]
            a[p, g + 8] = far[np.random.randint(len(far))]
    return np.exp2(a.ravel()).repeat(32)


def f64(x):
    return np.asarray(x).astype(np.float64)


def striped8(idx):
    return np.asarray(idx).reshape(8, -1, 16).transpose(0, 2, 1).reshape(128, -1).astype(np.uint16)


def unstriped8(offs):
    return offs.reshape(8, 16, -1).transpose(0, 2, 1).reshape(8, -1).astype(np.int64)


def pick8(x, idx, run):
    r = np.arange(len(x))
    return x[r[:, None], idx[r % (8 * run) // run]]


E2M1 = np.array([0.0, 0.5, 1.0, 1.5, 2.0, 3.0, 4.0, 6.0, -0.0, -0.5, -1.0, -1.5, -2.0, -3.0, -4.0, -6.0])


def pack_weight(w, fmt):
    k, n = w.shape
    w = f64(np.asarray(w, np.float32).astype(ml_dtypes.bfloat16)).reshape(k // 32, 32, n)
    amax = np.abs(w).max(1)
    if fmt == "e4m3":
        byte = np.frexp(amax)[1] - 1 + 127 - 7
    else:
        mant, ex = np.frexp(amax / 6.0)
        byte = np.where(mant > 0.5, ex, ex - 1) + 127
    byte = np.clip(np.where(amax > 0, byte, 1), 1, 254)
    scaled = (w * np.exp2(127.0 - byte)[:, None, :]).reshape(k, n).astype(np.float32)
    by_word = np.ascontiguousarray(scaled.reshape(k // 512, 128, 4, n).transpose(0, 1, 3, 2))
    if fmt == "e4m3":
        words = by_word.astype(ml_dtypes.float8_e4m3fn).view(np.uint8)
    else:
        c = by_word.astype(ml_dtypes.float4_e2m1fn).view(np.uint8) & 0xF
        words = (c[..., 0::2] | (c[..., 1::2] << 4)).reshape(k // 512, 128, 2 * n)
    return np.ascontiguousarray(words), np.ascontiguousarray(byte.astype(np.uint8).reshape(k // 512, 16, n))


def unpack_weight(words, scales, fmt):
    g, _, n = scales.shape
    words = np.ascontiguousarray(words).reshape(g, 128, n, -1)
    if fmt == "e4m3":
        vals = words.view(ml_dtypes.float8_e4m3fn).astype(np.float64)
    else:
        nib = np.empty((g, 128, n, 4), np.uint8)
        nib[..., 0::2] = words & 0xF
        nib[..., 1::2] = words >> 4
        vals = E2M1[nib]
    vals = vals * np.repeat(np.exp2(scales.astype(np.float64) - 127.0), 8, axis=1)[..., None]
    return vals.transpose(0, 1, 3, 2).reshape(g * 512, n)


D, K, T, U, I, Q = 512, 512, 1024, 1024, 512, 128


def setup_inputs():
    n = np.random.standard_normal
    idx = np.stack([np.random.permutation(T)[:I] for _ in range(8)])
    idx2 = np.stack([np.random.permutation(U)[:I] for _ in range(8)])
    idx3 = np.stack([np.random.permutation(T)[:I] for _ in range(8)])
    idx4 = np.stack([np.random.permutation(U)[:I] for _ in range(8)])
    fd = mx_kscale(D)
    fk = mx_kscale(K)
    wqp = pack_weight(n((D, K)) * 1.0 / np.sqrt(D) * fd[:, None] * fk, "e4m3")
    keysp = pack_weight(n((K, T)) * 1.0 / np.sqrt(K) / fk[:, None], "e2m1")
    notesp = pack_weight(n((D, U)) * 1.0 / np.sqrt(D) * fd[:, None], "e4m3")
    return {
        "states": (n((D, Q)) * 0.95 / fd[:, None]).astype(np.float32),
        "wq_words": wqp[0],
        "wq_scales": wqp[1],
        "keys_words": keysp[0],
        "keys_scales": keysp[1],
        "notes_words": notesp[0],
        "notes_scales": notesp[1],
        "offs": striped8(idx),
        "offs2": striped8(idx2),
        "offs3": striped8(idx3),
        "offs4": striped8(idx4),
    }


def reference(states, wq_words, wq_scales, keys_words, keys_scales, notes_words, notes_scales, offs, offs2, offs3, offs4):
    idx = unstriped8(offs)
    idx2 = unstriped8(offs2)
    idx3 = unstriped8(offs3)
    idx4 = unstriped8(offs4)
    wqu = unpack_weight(wq_words, wq_scales, "e4m3")
    keysu = unpack_weight(keys_words, keys_scales, "e2m1")
    notesu = unpack_weight(notes_words, notes_scales, "e4m3")
    statesq = mxq(f64(states), 0, "e4m3")
    qv = wqu.T @ statesq
    qvq = mxq(qv, 0, "e4m3")
    a = qvq.T @ keysu
    b = statesq.T @ notesu
    w = np.maximum(pick8(a, idx, 16), pick8(b, idx2, 16))
    v = np.minimum(pick8(a, idx3, 16), pick8(b, idx4, 16))
    f1 = np.zeros((Q, T))
    f1[np.arange(Q)[:, None], idx3[np.arange(Q) % 128 // 16]] = w
    cc = a + f1
    y = pick8(cc, idx, 16) - v
    return y

@@ -1,0 +1,185 @@
+from contextlib import ExitStack
+
+import concourse.mybir as mybir
+
+D, K, T, U, SLOTS, Q = 512, 512, 1024, 1024, 512, 128
+FLOPS = 2 * Q * (D * K + K * T + D * U)
+
+F32 = mybir.dt.float32
+BF16 = mybir.dt.bfloat16
+I32 = mybir.dt.int32
+U32 = mybir.dt.uint32
+U16 = mybir.dt.uint16
+U8 = mybir.dt.uint8
+FP8X4 = mybir.dt.float8_e4m3fn_x4
+FP4X4 = mybir.dt.float4_e2m1fn_x4
+ALU = mybir.AluOpType
+COPY = mybir.ActivationFunctionType.Copy
+
+P = 128
+PACK = 4
+HALF = SLOTS // 2
+A_COLS = 256
+B_COLS = 256
+Q_VECTOR = 96
+
+
+def load_scale_rows(queue, plane, rows, quadrants):
+    for g in quadrants:
+        queue.dma_start(out=plane[32 * g : 32 * g + 4, :].bitcast(I32), in_=rows[4 * g : 4 * g + 4, :].bitcast(I32))
+
+
+def tile_attend_spread_madeside_kernel(
+    tc, states, wq_words, wq_scales, keys_words, keys_scales, notes_words, notes_scales, offs, offs2, offs3, offs4, out
+):
+    nc = tc.nc
+    with ExitStack() as ctx:
+        lists = ctx.enter_context(tc.tile_pool(name="lists", bufs=1))
+        sb = ctx.enter_context(tc.tile_pool(name="sb", bufs=1))
+        ps = ctx.enter_context(tc.psum_pool(name="ps", bufs=1))
+
+        idx1 = lists.tile([P, SLOTS // 16], U16, name="idx1")
+        idx2 = lists.tile([P, SLOTS // 16], U16, name="idx2")
+        idx3 = lists.tile([P, SLOTS // 16], U16, name="idx3")
+        idx4 = lists.tile([P, SLOTS // 16], U16, name="idx4")
+
+        def half(lst, h):
+            return lst[:, h * (HALF // 16) : (h + 1) * (HALF // 16)]
+
+        wq_plane = sb.tile([P, K], U8, name="wq_plane", align_bytes=64)
+        notes_plane = sb.tile([P, U], U8, name="notes_plane", align_bytes=64)
+        keys_plane = sb.tile([P, T], U8, name="keys_plane", align_bytes=64)
+        nc.vector.memset(keys_plane[:].bitcast(U32), 0)
+        nc.vector.memset(notes_plane[:].bitcast(U32), 0)
+
+        st_raw = sb.tile([P, PACK, Q], F32, name="st_raw", align_bytes=64)
+        wq_raw = sb.tile([P, K], U32, name="wq_raw", tag="wq_then_f1", align_bytes=64)
+        notes_codes = sb.tile([P, U], U32, name="notes_codes", align_bytes=64)
+        keys_codes = sb.tile([P, 2 * T], U8, name="keys_codes", align_bytes=64)
+
+        nc.scalar.dma_start(out=st_raw[:], in_=states.rearrange("(p j) q -> p j q", j=PACK))
+        for g in range(4):
+            nc.sync.dma_start(
+                out=wq_plane[32 * g : 32 * g + 32, :].bitcast(I32),
+                in_=wq_scales[0, 4 * g : 4 * g + 4, :].bitcast(I32).partition_broadcast(8),
+            )
+        nc.sync.dma_start(out=wq_raw[:].bitcast(I32), in_=wq_words[0].rearrange("p n t -> p (n t)").bitcast(I32))
+        load_scale_rows(nc.gpsimd, keys_plane, keys_scales[0], (2, 3))
+        load_scale_rows(nc.sync, notes_plane, notes_scales[0], (0,))
+        nc.sync.dma_start(out=notes_codes[:].bitcast(I32), in_=notes_words[0].rearrange("p n t -> p (n t)").bitcast(I32))
+        load_scale_rows(nc.sync, notes_plane, notes_scales[0], (1, 2, 3))
+        nc.sync.dma_start(out=keys_codes[:].bitcast(I32), in_=keys_words[0].bitcast(I32))
+        load_scale_rows(nc.sync, keys_plane, keys_scales[0], (0, 1))
+        nc.sync.dma_start(idx2[:], offs2)
+        nc.sync.dma_start(idx1[:], offs)
+        nc.sync.dma_start(idx3[:], offs3)
+        nc.sync.dma_start(idx4[:], offs4)
+
+        st_bf = sb.tile([P, Q, PACK], BF16, name="st_bf", align_bytes=64)
+        nc.scalar.activation(
+            st_bf[:, Q_VECTOR:, :].rearrange("p (c i) t -> p c t i", i=4),
+            st_raw[:, :, Q_VECTOR:].rearrange("p t (c i) -> p c t i", i=4),
+            COPY,
+        )
+        wq_plane_dealt = sb.tile([P, PACK, P], U8, name="wq_plane_dealt", align_bytes=64)
+        nc.vector.tensor_copy(out=wq_plane_dealt[:], in_=wq_plane[:].rearrange("p (m j) -> p j m", j=PACK))
+        nc.vector.tensor_copy(
+            out=st_bf[:, :Q_VECTOR, :].rearrange("p (c i) t -> p c t i", i=4),
+            in_=st_raw[:, :, :Q_VECTOR].rearrange("p t (c i) -> p c t i", i=4),
+        )
+        st_codes = sb.tile([P, Q], U32, name="st_codes", align_bytes=64)
+        st_plane = sb.tile([P, Q], U8, name="st_plane", align_bytes=64)
+        nc.vector.quantize_mx(out=st_codes[:].bitcast(FP8X4), scales=st_plane[:], in_=st_bf[:].rearrange("p q t -> p (q t)"))
+
+        wq_lo = sb.tile([P, 2, P], U32, name="wq_lo", align_bytes=64)
+        wq_hi = sb.tile([P, 2, P], U32, name="wq_hi", align_bytes=64)
+        wq_by_j = wq_raw[:].rearrange("p (m j) -> p j m", j=PACK)
+        nc.scalar.copy(out=wq_lo[:], in_=wq_by_j[:, 0:2, :])
+        nc.vector.tensor_copy(out=wq_hi[:], in_=wq_by_j[:, 2:4, :])
+
+        f1 = sb.tile([P, T], F32, name="f1", tag="wq_then_f1", align_bytes=64)
+        nc.vector.memset(f1[:], 0.0)
+
+        qv_ps = [ps.tile([P, 2, Q], F32, name="qv_ps%d" % u, tag="bank%d" % u) for u in range(2)]
+        for j in range(PACK):
+            src = wq_lo if j < 2 else wq_hi
+            nc.tensor.matmul_mx(
+                out=qv_ps[j // 2][:, j % 2, :],
+                lhsT=src[:, j % 2, :].bitcast(FP8X4),
+                lhsT_scale=wq_plane_dealt[:, j, :],
+                rhs=st_codes[:].bitcast(FP8X4),
+                rhs_scale=st_plane[:],
+                start=True,
+                stop=True,
+            )
+
+        qv_bf = sb.tile([P, Q, PACK], BF16, name="qv_bf", align_bytes=64)
+        nc.scalar.copy(out=qv_bf[:, :, 0:2], in_=qv_ps[0][:].rearrange("p j q -> p q j"))
+        nc.vector.tensor_copy(out=qv_bf[:, :, 2:4], in_=qv_ps[1][:].rearrange("p j q -> p q j"))
+
+        b_sb = sb.tile([P, U], F32, name="b_sb", align_bytes=64)
+        for c in range(U // B_COLS):
+            cols = slice(c * B_COLS, (c + 1) * B_COLS)
+            b_ps = ps.tile([P, B_COLS], F32, name="b_ps%d" % c)
+            nc.tensor.matmul_mx(
+                out=b_ps[:],
+                lhsT=st_codes[:].bitcast(FP8X4),
+                lhsT_scale=st_plane[:],
+                rhs=notes_codes[:, cols].bitcast(FP8X4),
+                rhs_scale=notes_plane[:, cols],
+                start=True,
+                stop=True,
+            )
+            nc.scalar.copy(out=b_sb[:, cols], in_=b_ps[:])
+
+        qv_codes = sb.tile([P, Q], U32, name="qv_codes", align_bytes=64)
+        qv_plane = sb.tile([P, Q], U8, name="qv_plane", align_bytes=64)
+        nc.vector.quantize_mx(out=qv_codes[:].bitcast(FP8X4), scales=qv_plane[:], in_=qv_bf[:].rearrange("p q t -> p (q t)"))
+
+        a_sb = sb.tile([P, T], F32, name="a_sb", align_bytes=64)
+        for c in range(T // A_COLS):
+            cols = slice(c * A_COLS, (c + 1) * A_COLS)
+            a_ps = ps.tile([P, A_COLS], F32, name="a_ps%d" % c, tag="bank%d" % ((c + 2) % 4))
+            nc.tensor.matmul_mx(
+                out=a_ps[:],
+                lhsT=qv_codes[:].bitcast(FP8X4),
+                lhsT_scale=qv_plane[:],
+                rhs=keys_codes[:, 2 * c * A_COLS : 2 * (c + 1) * A_COLS].bitcast(FP4X4),
+                rhs_scale=keys_plane[:, cols],
+                start=True,
+                stop=True,
+            )
+            nc.vector.tensor_copy(out=a_sb[:, cols], in_=a_ps[:])
+
+        b2 = [sb.tile([P, HALF], F32, name="b2_%d" % h) for h in range(2)]
+        a1 = [sb.tile([P, HALF], F32, name="a1_%d" % h) for h in range(2)]
+        w = [sb.tile([P, HALF], F32, name="w%d" % h, tag="w%d" % h) for h in range(2)]
+        a3 = sb.tile([P, SLOTS], F32, name="a3")
+        b4 = sb.tile([P, SLOTS], F32, name="b4")
+        for h in range(2):
+            nc.scalar.activation(b2[h][:], b_sb[:].indirect(half(idx2, h)), COPY)
+        nc.vector.tensor_copy(a1[0][:], a_sb[:].indirect(half(idx1, 0)))
+        nc.scalar.activation(a1[1][:], a_sb[:].indirect(half(idx1, 1)), COPY)
+        nc.scalar.activation(a3[:], a_sb[:].indirect(idx3[:]), COPY)
+        nc.scalar.activation(b4[:], b_sb[:].indirect(idx4[:]), COPY)
+
+        for h in range(2):
+            nc.vector.tensor_tensor(w[h][:], a1[h][:], b2[h][:], ALU.max)
+        for h in range(2):
+            nc.vector.tensor_copy(f1[:].indirect(half(idx3, h)), w[h][:])
+
+        v0 = sb.tile([P, HALF], F32, name="v0", tag="w0")
+        v1 = sb.tile([P, HALF], F32, name="v1")
+        cc = sb.tile([P, T], F32, name="cc")
+        nc.vector.tensor_tensor(v0[:], a3[:, :HALF], b4[:, :HALF], ALU.min)
+        nc.vector.tensor_tensor(cc[:], a_sb[:], f1[:], ALU.add)
+        nc.vector.tensor_tensor(v1[:], a3[:, HALF:], b4[:, HALF:], ALU.min)
+
+        y0 = sb.tile([P, HALF], F32, name="y0")
+        y1 = sb.tile([P, HALF], F32, name="y1")
+        c1 = sb.tile([P, HALF], F32, name="c1")
+        nc.scalar.activation(c1[:], cc[:].indirect(half(idx1, 1)), COPY)
+        nc.vector.tensor_tensor(y0[:], cc[:].indirect(half(idx1, 0)), v0[:], ALU.subtract)
+        nc.sync.dma_start(out=out[:, :HALF], in_=y0[:])
+        nc.vector.tensor_tensor(y1[:], c1[:], v1[:], ALU.subtract)
+        nc.sync.dma_start(out=out[:, HALF:], in_=y1[:])

@@ -19,9 +19,11 @@ COPY = mybir.ActivationFunctionType.Copy
 P = 128
 PACK = 4
 HALF = SLOTS // 2
-A_COLS = 256
+A_PIECES = ((0, 256), (256, 512), (512, 768), (768, 896), (896, 1024))
 B_COLS = 256
 Q_VECTOR = 96
+DEAL_VECTOR = 24
+CC_VECTOR = 3
 
 
 def load_scale_rows(queue, plane, rows, quadrants):
@@ -49,8 +51,8 @@ def tile_attend_spread_madeside_kernel(
         wq_plane = sb.tile([P, K], U8, name="wq_plane", align_bytes=64)
         notes_plane = sb.tile([P, U], U8, name="notes_plane", align_bytes=64)
         keys_plane = sb.tile([P, T], U8, name="keys_plane", align_bytes=64)
-        nc.vector.memset(keys_plane[:].bitcast(U32), 0)
         nc.vector.memset(notes_plane[:].bitcast(U32), 0)
+        nc.vector.memset(keys_plane[:].bitcast(U32), 0)
 
         st_raw = sb.tile([P, PACK, Q], F32, name="st_raw", align_bytes=64)
         wq_raw = sb.tile([P, K], U32, name="wq_raw", tag="wq_then_f1", align_bytes=64)
@@ -64,12 +66,13 @@ def tile_attend_spread_madeside_kernel(
                 in_=wq_scales[0, 4 * g : 4 * g + 4, :].bitcast(I32).partition_broadcast(8),
             )
         nc.sync.dma_start(out=wq_raw[:].bitcast(I32), in_=wq_words[0].rearrange("p n t -> p (n t)").bitcast(I32))
-        load_scale_rows(nc.gpsimd, keys_plane, keys_scales[0], (2, 3))
+        load_scale_rows(nc.gpsimd, notes_plane, notes_scales[0], (3,))
+        load_scale_rows(nc.gpsimd, keys_plane, keys_scales[0], (3,))
         load_scale_rows(nc.sync, notes_plane, notes_scales[0], (0,))
         nc.sync.dma_start(out=notes_codes[:].bitcast(I32), in_=notes_words[0].rearrange("p n t -> p (n t)").bitcast(I32))
-        load_scale_rows(nc.sync, notes_plane, notes_scales[0], (1, 2, 3))
+        load_scale_rows(nc.sync, notes_plane, notes_scales[0], (1, 2))
         nc.sync.dma_start(out=keys_codes[:].bitcast(I32), in_=keys_words[0].bitcast(I32))
-        load_scale_rows(nc.sync, keys_plane, keys_scales[0], (0, 1))
+        load_scale_rows(nc.sync, keys_plane, keys_scales[0], (0, 1, 2))
         nc.sync.dma_start(idx2[:], offs2)
         nc.sync.dma_start(idx1[:], offs)
         nc.sync.dma_start(idx3[:], offs3)
@@ -91,21 +94,20 @@ def tile_attend_spread_madeside_kernel(
         st_plane = sb.tile([P, Q], U8, name="st_plane", align_bytes=64)
         nc.vector.quantize_mx(out=st_codes[:].bitcast(FP8X4), scales=st_plane[:], in_=st_bf[:].rearrange("p q t -> p (q t)"))
 
-        wq_lo = sb.tile([P, 2, P], U32, name="wq_lo", align_bytes=64)
-        wq_hi = sb.tile([P, 2, P], U32, name="wq_hi", align_bytes=64)
-        wq_by_j = wq_raw[:].rearrange("p (m j) -> p j m", j=PACK)
-        nc.scalar.copy(out=wq_lo[:], in_=wq_by_j[:, 0:2, :])
-        nc.vector.tensor_copy(out=wq_hi[:], in_=wq_by_j[:, 2:4, :])
+        wq_dealt = sb.tile([P, PACK, P], U32, name="wq_dealt", align_bytes=64)
+        deal_to = wq_dealt[:].rearrange("p j (c i) -> p c j i", i=4)
+        deal_from = wq_raw[:].rearrange("p (c i j) -> p c j i", i=4, j=PACK)
+        nc.scalar.copy(out=deal_to[:, DEAL_VECTOR:], in_=deal_from[:, DEAL_VECTOR:])
+        nc.vector.tensor_copy(out=deal_to[:, :DEAL_VECTOR], in_=deal_from[:, :DEAL_VECTOR])
 
         f1 = sb.tile([P, T], F32, name="f1", tag="wq_then_f1", align_bytes=64)
         nc.vector.memset(f1[:], 0.0)
 
         qv_ps = [ps.tile([P, 2, Q], F32, name="qv_ps%d" % u, tag="bank%d" % u) for u in range(2)]
         for j in range(PACK):
-            src = wq_lo if j < 2 else wq_hi
             nc.tensor.matmul_mx(
                 out=qv_ps[j // 2][:, j % 2, :],
-                lhsT=src[:, j % 2, :].bitcast(FP8X4),
+                lhsT=wq_dealt[:, j, :].bitcast(FP8X4),
                 lhsT_scale=wq_plane_dealt[:, j, :],
                 rhs=st_codes[:].bitcast(FP8X4),
                 rhs_scale=st_plane[:],
@@ -120,7 +122,7 @@ def tile_attend_spread_madeside_kernel(
         b_sb = sb.tile([P, U], F32, name="b_sb", align_bytes=64)
         for c in range(U // B_COLS):
             cols = slice(c * B_COLS, (c + 1) * B_COLS)
-            b_ps = ps.tile([P, B_COLS], F32, name="b_ps%d" % c)
+            b_ps = ps.tile([P, B_COLS], F32, name="b_ps%d" % c, tag="bank%d" % (2 + c))
             nc.tensor.matmul_mx(
                 out=b_ps[:],
                 lhsT=st_codes[:].bitcast(FP8X4),
@@ -137,43 +139,50 @@ def tile_attend_spread_madeside_kernel(
         nc.vector.quantize_mx(out=qv_codes[:].bitcast(FP8X4), scales=qv_plane[:], in_=qv_bf[:].rearrange("p q t -> p (q t)"))
 
         a_sb = sb.tile([P, T], F32, name="a_sb", align_bytes=64)
-        for c in range(T // A_COLS):
-            cols = slice(c * A_COLS, (c + 1) * A_COLS)
-            a_ps = ps.tile([P, A_COLS], F32, name="a_ps%d" % c, tag="bank%d" % ((c + 2) % 4))
+        a_banks = []
+        for c, (lo, hi) in enumerate(A_PIECES):
+            cols = slice(lo, hi)
+            a_ps = ps.tile([P, hi - lo], F32, name="a_ps%d" % c, tag="bank%d" % ((6 + c) % 8))
             nc.tensor.matmul_mx(
                 out=a_ps[:],
                 lhsT=qv_codes[:].bitcast(FP8X4),
                 lhsT_scale=qv_plane[:],
-                rhs=keys_codes[:, 2 * c * A_COLS : 2 * (c + 1) * A_COLS].bitcast(FP4X4),
+                rhs=keys_codes[:, 2 * lo : 2 * hi].bitcast(FP4X4),
                 rhs_scale=keys_plane[:, cols],
                 start=True,
                 stop=True,
             )
             nc.vector.tensor_copy(out=a_sb[:, cols], in_=a_ps[:])
+            a_banks.append(a_ps)
 
-        b2 = [sb.tile([P, HALF], F32, name="b2_%d" % h) for h in range(2)]
-        a1 = [sb.tile([P, HALF], F32, name="a1_%d" % h) for h in range(2)]
-        w = [sb.tile([P, HALF], F32, name="w%d" % h, tag="w%d" % h) for h in range(2)]
-        a3 = sb.tile([P, SLOTS], F32, name="a3")
-        b4 = sb.tile([P, SLOTS], F32, name="b4")
+        b2 = [sb.tile([P, HALF], F32, name="b2_%d" % h, tag="b2_%d" % h) for h in range(2)]
+        a1 = [sb.tile([P, HALF], F32, name="a1_%d" % h, tag="a1_%d" % h) for h in range(2)]
+        w = sb.tile([P, SLOTS], F32, name="w", tag="w")
+        a3 = [sb.tile([P, HALF], F32, name="a3_%d" % h) for h in range(2)]
         for h in range(2):
             nc.scalar.activation(b2[h][:], b_sb[:].indirect(half(idx2, h)), COPY)
         nc.vector.tensor_copy(a1[0][:], a_sb[:].indirect(half(idx1, 0)))
         nc.scalar.activation(a1[1][:], a_sb[:].indirect(half(idx1, 1)), COPY)
-        nc.scalar.activation(a3[:], a_sb[:].indirect(idx3[:]), COPY)
-        nc.scalar.activation(b4[:], b_sb[:].indirect(idx4[:]), COPY)
+        for h in range(2):
+            nc.scalar.activation(a3[h][:], a_sb[:].indirect(half(idx3, h)), COPY)
 
         for h in range(2):
-            nc.vector.tensor_tensor(w[h][:], a1[h][:], b2[h][:], ALU.max)
+            nc.vector.tensor_tensor(w[:, h * HALF : (h + 1) * HALF], a1[h][:], b2[h][:], ALU.max)
+        nc.vector.tensor_copy(f1[:].indirect(idx3[:]), w[:])
+        b4 = [sb.tile([P, HALF], F32, name="b4_%d" % h, tag=("a1_0", "b2_0")[h]) for h in range(2)]
         for h in range(2):
-            nc.vector.tensor_copy(f1[:].indirect(half(idx3, h)), w[h][:])
+            nc.scalar.activation(b4[h][:], b_sb[:].indirect(half(idx4, h)), COPY)
 
-        v0 = sb.tile([P, HALF], F32, name="v0", tag="w0")
-        v1 = sb.tile([P, HALF], F32, name="v1")
+        v0 = sb.tile([P, HALF], F32, name="v0", tag="a1_1")
+        v1 = sb.tile([P, HALF], F32, name="v1", tag="w")
         cc = sb.tile([P, T], F32, name="cc")
-        nc.vector.tensor_tensor(v0[:], a3[:, :HALF], b4[:, :HALF], ALU.min)
-        nc.vector.tensor_tensor(cc[:], a_sb[:], f1[:], ALU.add)
-        nc.vector.tensor_tensor(v1[:], a3[:, HALF:], b4[:, HALF:], ALU.min)
+        nc.vector.tensor_tensor(v0[:], a3[0][:], b4[0][:], ALU.min)
+        split = A_PIECES[CC_VECTOR][0]
+        nc.gpsimd.tensor_tensor(cc[:, split:], a_sb[:, split:], f1[:, split:], ALU.add)
+        for c in range(CC_VECTOR):
+            lo, hi = A_PIECES[c]
+            nc.vector.tensor_tensor(cc[:, lo:hi], a_banks[c][:], f1[:, lo:hi], ALU.add)
+        nc.vector.tensor_tensor(v1[:], a3[1][:], b4[1][:], ALU.min)
 
         y0 = sb.tile([P, HALF], F32, name="y0")
         y1 = sb.tile([P, HALF], F32, name="y1")

@@ -21,9 +21,10 @@ PACK = 4
 HALF = SLOTS // 2
 A_PIECES = ((0, 256), (256, 512), (512, 768), (768, 896), (896, 1024))
 B_COLS = 256
-Q_VECTOR = 96
-DEAL_VECTOR = 24
+Q_VECTOR = 64
+DEAL_VECTOR = 18
 CC_VECTOR = 3
+A_VECTOR = (2, 4)
 
 
 def load_scale_rows(queue, plane, rows, quadrants):
@@ -55,7 +56,7 @@ def tile_attend_spread_madeside_kernel(
         nc.vector.memset(keys_plane[:].bitcast(U32), 0)
 
         st_raw = sb.tile([P, PACK, Q], F32, name="st_raw", align_bytes=64)
-        wq_raw = sb.tile([P, K], U32, name="wq_raw", tag="wq_then_f1", align_bytes=64)
+        wq_raw = sb.tile([P, K], U32, name="wq_raw", align_bytes=64)
         notes_codes = sb.tile([P, U], U32, name="notes_codes", align_bytes=64)
         keys_codes = sb.tile([P, 2 * T], U8, name="keys_codes", align_bytes=64)
 
@@ -100,8 +101,6 @@ def tile_attend_spread_madeside_kernel(
         nc.scalar.copy(out=deal_to[:, DEAL_VECTOR:], in_=deal_from[:, DEAL_VECTOR:])
         nc.vector.tensor_copy(out=deal_to[:, :DEAL_VECTOR], in_=deal_from[:, :DEAL_VECTOR])
 
-        f1 = sb.tile([P, T], F32, name="f1", tag="wq_then_f1", align_bytes=64)
-        nc.vector.memset(f1[:], 0.0)
 
         qv_ps = [ps.tile([P, 2, Q], F32, name="qv_ps%d" % u, tag="bank%d" % u) for u in range(2)]
         for j in range(PACK):
@@ -115,14 +114,14 @@ def tile_attend_spread_madeside_kernel(
                 stop=True,
             )
 
-        qv_bf = sb.tile([P, Q, PACK], BF16, name="qv_bf", align_bytes=64)
+        qv_bf = sb.tile([P, Q, PACK], BF16, name="qv_bf", tag="qv_then_f1", align_bytes=64)
         nc.scalar.copy(out=qv_bf[:, :, 0:2], in_=qv_ps[0][:].rearrange("p j q -> p q j"))
         nc.vector.tensor_copy(out=qv_bf[:, :, 2:4], in_=qv_ps[1][:].rearrange("p j q -> p q j"))
 
         b_sb = sb.tile([P, U], F32, name="b_sb", align_bytes=64)
-        for c in range(U // B_COLS):
-            cols = slice(c * B_COLS, (c + 1) * B_COLS)
-            b_ps = ps.tile([P, B_COLS], F32, name="b_ps%d" % c, tag="bank%d" % (2 + c))
+        for c, (lo, hi) in enumerate(A_PIECES):
+            cols = slice(lo, hi)
+            b_ps = ps.tile([P, hi - lo], F32, name="b_ps%d" % c, tag="bank%d" % (2 + c))
             nc.tensor.matmul_mx(
                 out=b_ps[:],
                 lhsT=st_codes[:].bitcast(FP8X4),
@@ -132,17 +131,22 @@ def tile_attend_spread_madeside_kernel(
                 start=True,
                 stop=True,
             )
-            nc.scalar.copy(out=b_sb[:, cols], in_=b_ps[:])
+            if hi < U:
+                nc.scalar.copy(out=b_sb[:, cols], in_=b_ps[:])
 
-        qv_codes = sb.tile([P, Q], U32, name="qv_codes", align_bytes=64)
+        qv_codes = sb.tile([P, Q], U32, name="qv_codes", tag="b2_1", align_bytes=64)
         qv_plane = sb.tile([P, Q], U8, name="qv_plane", align_bytes=64)
         nc.vector.quantize_mx(out=qv_codes[:].bitcast(FP8X4), scales=qv_plane[:], in_=qv_bf[:].rearrange("p q t -> p (q t)"))
+
+        nc.vector.tensor_copy(out=b_sb[:, cols], in_=b_ps[:])
+        f1 = sb.tile([P, T], F32, name="f1", tag="qv_then_f1", align_bytes=64)
+        nc.gpsimd.memset(f1[:], 0.0)
 
         a_sb = sb.tile([P, T], F32, name="a_sb", align_bytes=64)
         a_banks = []
         for c, (lo, hi) in enumerate(A_PIECES):
             cols = slice(lo, hi)
-            a_ps = ps.tile([P, hi - lo], F32, name="a_ps%d" % c, tag="bank%d" % ((6 + c) % 8))
+            a_ps = ps.tile([P, hi - lo], F32, name="a_ps%d" % c, tag="bank%d" % ((7 + c) % 8))
             nc.tensor.matmul_mx(
                 out=a_ps[:],
                 lhsT=qv_codes[:].bitcast(FP8X4),
@@ -152,15 +156,18 @@ def tile_attend_spread_madeside_kernel(
                 start=True,
                 stop=True,
             )
-            nc.vector.tensor_copy(out=a_sb[:, cols], in_=a_ps[:])
+            if c in A_VECTOR:
+                nc.vector.tensor_copy(out=a_sb[:, cols], in_=a_ps[:])
+            else:
+                nc.scalar.copy(out=a_sb[:, cols], in_=a_ps[:])
             a_banks.append(a_ps)
 
-        b2 = [sb.tile([P, HALF], F32, name="b2_%d" % h, tag="b2_%d" % h) for h in range(2)]
-        a1 = [sb.tile([P, HALF], F32, name="a1_%d" % h, tag="a1_%d" % h) for h in range(2)]
+        b2 = [sb.tile([P, HALF], F32, name="b2_%d" % h, tag="b2_%d" % h, align_bytes=64) for h in range(2)]
+        a1 = [sb.tile([P, HALF], F32, name="a1_%d" % h, tag="a1_%d" % h, align_bytes=64) for h in range(2)]
         w = sb.tile([P, SLOTS], F32, name="w", tag="w")
         a3 = [sb.tile([P, HALF], F32, name="a3_%d" % h) for h in range(2)]
-        for h in range(2):
-            nc.scalar.activation(b2[h][:], b_sb[:].indirect(half(idx2, h)), COPY)
+        nc.vector.tensor_copy(b2[0][:], b_sb[:].indirect(half(idx2, 0)))
+        nc.scalar.activation(b2[1][:], b_sb[:].indirect(half(idx2, 1)), COPY)
         nc.vector.tensor_copy(a1[0][:], a_sb[:].indirect(half(idx1, 0)))
         nc.scalar.activation(a1[1][:], a_sb[:].indirect(half(idx1, 1)), COPY)
         for h in range(2):
@@ -169,19 +176,19 @@ def tile_attend_spread_madeside_kernel(
         for h in range(2):
             nc.vector.tensor_tensor(w[:, h * HALF : (h + 1) * HALF], a1[h][:], b2[h][:], ALU.max)
         nc.vector.tensor_copy(f1[:].indirect(idx3[:]), w[:])
-        b4 = [sb.tile([P, HALF], F32, name="b4_%d" % h, tag=("a1_0", "b2_0")[h]) for h in range(2)]
+        b4 = [sb.tile([P, HALF], F32, name="b4_%d" % h, tag=("a1_0", "b2_0")[h], align_bytes=64) for h in range(2)]
         for h in range(2):
             nc.scalar.activation(b4[h][:], b_sb[:].indirect(half(idx4, h)), COPY)
 
-        v0 = sb.tile([P, HALF], F32, name="v0", tag="a1_1")
+        v0 = sb.tile([P, HALF], F32, name="v0", tag="a1_1", align_bytes=64)
         v1 = sb.tile([P, HALF], F32, name="v1", tag="w")
         cc = sb.tile([P, T], F32, name="cc")
-        nc.vector.tensor_tensor(v0[:], a3[0][:], b4[0][:], ALU.min)
         split = A_PIECES[CC_VECTOR][0]
         nc.gpsimd.tensor_tensor(cc[:, split:], a_sb[:, split:], f1[:, split:], ALU.add)
         for c in range(CC_VECTOR):
             lo, hi = A_PIECES[c]
             nc.vector.tensor_tensor(cc[:, lo:hi], a_banks[c][:], f1[:, lo:hi], ALU.add)
+        nc.vector.tensor_tensor(v0[:], a3[0][:], b4[0][:], ALU.min)
         nc.vector.tensor_tensor(v1[:], a3[1][:], b4[1][:], ALU.min)
 
         y0 = sb.tile([P, HALF], F32, name="y0")

@@ -56,7 +56,7 @@ def tile_attend_spread_madeside_kernel(
         nc.vector.memset(keys_plane[:].bitcast(U32), 0)
 
         st_raw = sb.tile([P, PACK, Q], F32, name="st_raw", align_bytes=64)
-        wq_raw = sb.tile([P, K], U32, name="wq_raw", align_bytes=64)
+        wq_raw = sb.tile([P, K], U32, name="wq_raw", tag="wq_then_f1", align_bytes=64)
         notes_codes = sb.tile([P, U], U32, name="notes_codes", align_bytes=64)
         keys_codes = sb.tile([P, 2 * T], U8, name="keys_codes", align_bytes=64)
 
@@ -102,6 +102,9 @@ def tile_attend_spread_madeside_kernel(
         nc.vector.tensor_copy(out=deal_to[:, :DEAL_VECTOR], in_=deal_from[:, :DEAL_VECTOR])
 
 
+        f1 = sb.tile([P, T], F32, name="f1", tag="wq_then_f1", align_bytes=64)
+        nc.vector.memset(f1[:].bitcast(U32), 0)
+
         qv_ps = [ps.tile([P, 2, Q], F32, name="qv_ps%d" % u, tag="bank%d" % u) for u in range(2)]
         for j in range(PACK):
             nc.tensor.matmul_mx(
@@ -114,7 +117,7 @@ def tile_attend_spread_madeside_kernel(
                 stop=True,
             )
 
-        qv_bf = sb.tile([P, Q, PACK], BF16, name="qv_bf", tag="qv_then_f1", align_bytes=64)
+        qv_bf = sb.tile([P, Q, PACK], BF16, name="qv_bf", align_bytes=64)
         nc.scalar.copy(out=qv_bf[:, :, 0:2], in_=qv_ps[0][:].rearrange("p j q -> p q j"))
         nc.vector.tensor_copy(out=qv_bf[:, :, 2:4], in_=qv_ps[1][:].rearrange("p j q -> p q j"))
 
@@ -139,8 +142,6 @@ def tile_attend_spread_madeside_kernel(
         nc.vector.quantize_mx(out=qv_codes[:].bitcast(FP8X4), scales=qv_plane[:], in_=qv_bf[:].rearrange("p q t -> p (q t)"))
 
         nc.vector.tensor_copy(out=b_sb[:, cols], in_=b_ps[:])
-        f1 = sb.tile([P, T], F32, name="f1", tag="qv_then_f1", align_bytes=64)
-        nc.gpsimd.memset(f1[:], 0.0)
 
         a_sb = sb.tile([P, T], F32, name="a_sb", align_bytes=64)
         a_banks = []

from contextlib import ExitStack

import concourse.mybir as mybir

D, K, T, U, SLOTS, Q = 512, 512, 1024, 1024, 512, 128
FLOPS = 2 * Q * (D * K + K * T + D * U)

F32 = mybir.dt.float32
BF16 = mybir.dt.bfloat16
I32 = mybir.dt.int32
U32 = mybir.dt.uint32
U16 = mybir.dt.uint16
U8 = mybir.dt.uint8
FP8X4 = mybir.dt.float8_e4m3fn_x4
FP4X4 = mybir.dt.float4_e2m1fn_x4
ALU = mybir.AluOpType
COPY = mybir.ActivationFunctionType.Copy

P = 128
PACK = 4
HALF = SLOTS // 2
A_PIECES = ((0, 256), (256, 512), (512, 768), (768, 896), (896, 1024))
B_COLS = 256
Q_VECTOR = 64
DEAL_VECTOR = 18
CC_VECTOR = 3
A_VECTOR = (2, 4)


def load_scale_rows(queue, plane, rows, quadrants):
    for g in quadrants:
        queue.dma_start(out=plane[32 * g : 32 * g + 4, :].bitcast(I32), in_=rows[4 * g : 4 * g + 4, :].bitcast(I32))


def tile_attend_spread_madeside_kernel(
    tc, states, wq_words, wq_scales, keys_words, keys_scales, notes_words, notes_scales, offs, offs2, offs3, offs4, out
):
    nc = tc.nc
    with ExitStack() as ctx:
        lists = ctx.enter_context(tc.tile_pool(name="lists", bufs=1))
        sb = ctx.enter_context(tc.tile_pool(name="sb", bufs=1))
        ps = ctx.enter_context(tc.psum_pool(name="ps", bufs=1))

        idx1 = lists.tile([P, SLOTS // 16], U16, name="idx1")
        idx2 = lists.tile([P, SLOTS // 16], U16, name="idx2")
        idx3 = lists.tile([P, SLOTS // 16], U16, name="idx3")
        idx4 = lists.tile([P, SLOTS // 16], U16, name="idx4")

        def half(lst, h):
            return lst[:, h * (HALF // 16) : (h + 1) * (HALF // 16)]

        wq_plane = sb.tile([P, K], U8, name="wq_plane", align_bytes=64)
        notes_plane = sb.tile([P, U], U8, name="notes_plane", align_bytes=64)
        keys_plane = sb.tile([P, T], U8, name="keys_plane", align_bytes=64)
        nc.vector.memset(notes_plane[:].bitcast(U32), 0)
        nc.vector.memset(keys_plane[:].bitcast(U32), 0)

        st_raw = sb.tile([P, PACK, Q], F32, name="st_raw", align_bytes=64)
        wq_raw = sb.tile([P, K], U32, name="wq_raw", tag="wq_then_f1", align_bytes=64)
        notes_codes = sb.tile([P, U], U32, name="notes_codes", align_bytes=64)
        keys_codes = sb.tile([P, 2 * T], U8, name="keys_codes", align_bytes=64)

        nc.scalar.dma_start(out=st_raw[:], in_=states.rearrange("(p j) q -> p j q", j=PACK))
        for g in range(4):
            nc.sync.dma_start(
                out=wq_plane[32 * g : 32 * g + 32, :].bitcast(I32),
                in_=wq_scales[0, 4 * g : 4 * g + 4, :].bitcast(I32).partition_broadcast(8),
            )
        nc.sync.dma_start(out=wq_raw[:].bitcast(I32), in_=wq_words[0].rearrange("p n t -> p (n t)").bitcast(I32))
        load_scale_rows(nc.gpsimd, notes_plane, notes_scales[0], (3,))
        load_scale_rows(nc.gpsimd, keys_plane, keys_scales[0], (3,))
        load_scale_rows(nc.sync, notes_plane, notes_scales[0], (0,))
        nc.sync.dma_start(out=notes_codes[:].bitcast(I32), in_=notes_words[0].rearrange("p n t -> p (n t)").bitcast(I32))
        load_scale_rows(nc.sync, notes_plane, notes_scales[0], (1, 2))
        nc.sync.dma_start(out=keys_codes[:].bitcast(I32), in_=keys_words[0].bitcast(I32))
        load_scale_rows(nc.sync, keys_plane, keys_scales[0], (0, 1, 2))
        nc.sync.dma_start(idx2[:], offs2)
        nc.sync.dma_start(idx1[:], offs)
        nc.sync.dma_start(idx3[:], offs3)
        nc.sync.dma_start(idx4[:], offs4)

        st_bf = sb.tile([P, Q, PACK], BF16, name="st_bf", align_bytes=64)
        nc.scalar.activation(
            st_bf[:, Q_VECTOR:, :].rearrange("p (c i) t -> p c t i", i=4),
            st_raw[:, :, Q_VECTOR:].rearrange("p t (c i) -> p c t i", i=4),
            COPY,
        )
        wq_plane_dealt = sb.tile([P, PACK, P], U8, name="wq_plane_dealt", align_bytes=64)
        nc.vector.tensor_copy(out=wq_plane_dealt[:], in_=wq_plane[:].rearrange("p (m j) -> p j m", j=PACK))
        nc.vector.tensor_copy(
            out=st_bf[:, :Q_VECTOR, :].rearrange("p (c i) t -> p c t i", i=4),
            in_=st_raw[:, :, :Q_VECTOR].rearrange("p t (c i) -> p c t i", i=4),
        )
        st_codes = sb.tile([P, Q], U32, name="st_codes", align_bytes=64)
        st_plane = sb.tile([P, Q], U8, name="st_plane", align_bytes=64)
        nc.vector.quantize_mx(out=st_codes[:].bitcast(FP8X4), scales=st_plane[:], in_=st_bf[:].rearrange("p q t -> p (q t)"))

        wq_dealt = sb.tile([P, PACK, P], U32, name="wq_dealt", align_bytes=64)
        deal_to = wq_dealt[:].rearrange("p j (c i) -> p c j i", i=4)
        deal_from = wq_raw[:].rearrange("p (c i j) -> p c j i", i=4, j=PACK)
        nc.scalar.copy(out=deal_to[:, DEAL_VECTOR:], in_=deal_from[:, DEAL_VECTOR:])
        nc.vector.tensor_copy(out=deal_to[:, :DEAL_VECTOR], in_=deal_from[:, :DEAL_VECTOR])


        f1 = sb.tile([P, T], F32, name="f1", tag="wq_then_f1", align_bytes=64)
        nc.vector.memset(f1[:].bitcast(U32), 0)

        qv_ps = [ps.tile([P, 2, Q], F32, name="qv_ps%d" % u, tag="bank%d" % u) for u in range(2)]
        for j in range(PACK):
            nc.tensor.matmul_mx(
                out=qv_ps[j // 2][:, j % 2, :],
                lhsT=wq_dealt[:, j, :].bitcast(FP8X4),
                lhsT_scale=wq_plane_dealt[:, j, :],
                rhs=st_codes[:].bitcast(FP8X4),
                rhs_scale=st_plane[:],
                start=True,
                stop=True,
            )

        qv_bf = sb.tile([P, Q, PACK], BF16, name="qv_bf", align_bytes=64)
        nc.scalar.copy(out=qv_bf[:, :, 0:2], in_=qv_ps[0][:].rearrange("p j q -> p q j"))
        nc.vector.tensor_copy(out=qv_bf[:, :, 2:4], in_=qv_ps[1][:].rearrange("p j q -> p q j"))

        b_sb = sb.tile([P, U], F32, name="b_sb", align_bytes=64)
        for c, (lo, hi) in enumerate(A_PIECES):
            cols = slice(lo, hi)
            b_ps = ps.tile([P, hi - lo], F32, name="b_ps%d" % c, tag="bank%d" % (2 + c))
            nc.tensor.matmul_mx(
                out=b_ps[:],
                lhsT=st_codes[:].bitcast(FP8X4),
                lhsT_scale=st_plane[:],
                rhs=notes_codes[:, cols].bitcast(FP8X4),
                rhs_scale=notes_plane[:, cols],
                start=True,
                stop=True,
            )
            if hi < U:
                nc.scalar.copy(out=b_sb[:, cols], in_=b_ps[:])

        qv_codes = sb.tile([P, Q], U32, name="qv_codes", tag="b2_1", align_bytes=64)
        qv_plane = sb.tile([P, Q], U8, name="qv_plane", align_bytes=64)
        nc.vector.quantize_mx(out=qv_codes[:].bitcast(FP8X4), scales=qv_plane[:], in_=qv_bf[:].rearrange("p q t -> p (q t)"))

        nc.vector.tensor_copy(out=b_sb[:, cols], in_=b_ps[:])

        a_sb = sb.tile([P, T], F32, name="a_sb", align_bytes=64)
        a_banks = []
        for c, (lo, hi) in enumerate(A_PIECES):
            cols = slice(lo, hi)
            a_ps = ps.tile([P, hi - lo], F32, name="a_ps%d" % c, tag="bank%d" % ((7 + c) % 8))
            nc.tensor.matmul_mx(
                out=a_ps[:],
                lhsT=qv_codes[:].bitcast(FP8X4),
                lhsT_scale=qv_plane[:],
                rhs=keys_codes[:, 2 * lo : 2 * hi].bitcast(FP4X4),
                rhs_scale=keys_plane[:, cols],
                start=True,
                stop=True,
            )
            if c in A_VECTOR:
                nc.vector.tensor_copy(out=a_sb[:, cols], in_=a_ps[:])
            else:
                nc.scalar.copy(out=a_sb[:, cols], in_=a_ps[:])
            a_banks.append(a_ps)

        b2 = [sb.tile([P, HALF], F32, name="b2_%d" % h, tag="b2_%d" % h, align_bytes=64) for h in range(2)]
        a1 = [sb.tile([P, HALF], F32, name="a1_%d" % h, tag="a1_%d" % h, align_bytes=64) for h in range(2)]
        w = sb.tile([P, SLOTS], F32, name="w", tag="w")
        a3 = [sb.tile([P, HALF], F32, name="a3_%d" % h) for h in range(2)]
        nc.vector.tensor_copy(b2[0][:], b_sb[:].indirect(half(idx2, 0)))
        nc.scalar.activation(b2[1][:], b_sb[:].indirect(half(idx2, 1)), COPY)
        nc.vector.tensor_copy(a1[0][:], a_sb[:].indirect(half(idx1, 0)))
        nc.scalar.activation(a1[1][:], a_sb[:].indirect(half(idx1, 1)), COPY)
        for h in range(2):
            nc.scalar.activation(a3[h][:], a_sb[:].indirect(half(idx3, h)), COPY)

        for h in range(2):
            nc.vector.tensor_tensor(w[:, h * HALF : (h + 1) * HALF], a1[h][:], b2[h][:], ALU.max)
        nc.vector.tensor_copy(f1[:].indirect(idx3[:]), w[:])
        b4 = [sb.tile([P, HALF], F32, name="b4_%d" % h, tag=("a1_0", "b2_0")[h], align_bytes=64) for h in range(2)]
        for h in range(2):
            nc.scalar.activation(b4[h][:], b_sb[:].indirect(half(idx4, h)), COPY)

        v0 = sb.tile([P, HALF], F32, name="v0", tag="a1_1", align_bytes=64)
        v1 = sb.tile([P, HALF], F32, name="v1", tag="w")
        cc = sb.tile([P, T], F32, name="cc")
        split = A_PIECES[CC_VECTOR][0]
        nc.gpsimd.tensor_tensor(cc[:, split:], a_sb[:, split:], f1[:, split:], ALU.add)
        for c in range(CC_VECTOR):
            lo, hi = A_PIECES[c]
            nc.vector.tensor_tensor(cc[:, lo:hi], a_banks[c][:], f1[:, lo:hi], ALU.add)
        nc.vector.tensor_tensor(v0[:], a3[0][:], b4[0][:], ALU.min)
        nc.vector.tensor_tensor(v1[:], a3[1][:], b4[1][:], ALU.min)

        y0 = sb.tile([P, HALF], F32, name="y0")
        y1 = sb.tile([P, HALF], F32, name="y1")
        c1 = sb.tile([P, HALF], F32, name="c1")
        nc.scalar.activation(c1[:], cc[:].indirect(half(idx1, 1)), COPY)
        nc.vector.tensor_tensor(y0[:], cc[:].indirect(half(idx1, 0)), v0[:], ALU.subtract)
        nc.sync.dma_start(out=out[:, :HALF], in_=y0[:])
        nc.vector.tensor_tensor(y1[:], c1[:], v1[:], ALU.subtract)
        nc.sync.dma_start(out=out[:, HALF:], in_=y1[:])
